import numpy as np
import ml_dtypes


def mxq(x, axis, fmt="e4m3"):
    dtype, down = {"e4m3": (ml_dtypes.float8_e4m3fn, 7), "e5m2": (ml_dtypes.float8_e5m2, 14)}[fmt]
    v = np.moveaxis(np.asarray(x, np.float32).astype(ml_dtypes.bfloat16).astype(np.float64), axis, -1)
    blocks = v.reshape(v.shape[:-1] + (-1, 32))
    amax = np.abs(blocks).max(-1, keepdims=True)
    byte = np.maximum(np.where(amax > 0, np.frexp(amax)[1] - 1 + 127, 0) - down, 1)
    scale = np.exp2(byte - 127.0)
    codes = (blocks / scale).astype(np.float32).astype(dtype).astype(np.float64)
    return np.moveaxis((codes * scale).reshape(v.shape), -1, axis)


WIDE = False


def mx_kscale(k):
    if not WIDE:
        return np.ones(k)
    levels = np.array([10, -10, 5, -5, 0])
    if k % 512:
        return np.exp2(np.random.permutation(np.resize(levels, k // 32))).repeat(32)
    a = np.empty((k // 512, 16))
    for p in range(k // 512):
        a[p, :8] = np.random.permutation(np.resize(levels, 8))
        for g in range(8):
            far = levels[np.abs(levels - a[p, g]) >= 10]
            a[p, g + 8] = far[np.random.randint(len(far))]
    return np.exp2(a.ravel()).repeat(32)


def f64(x):
    return np.asarray(x).astype(np.float64)


def striped(idx):
    return np.tile(np.asarray(idx).reshape(-1, 16).T, (8, 1)).astype(np.uint16)


def unstriped(offs):
    return offs[:16].T.reshape(-1).astype(np.int64)


E2M1 = np.array([0.0, 0.5, 1.0, 1.5, 2.0, 3.0, 4.0, 6.0, -0.0, -0.5, -1.0, -1.5, -2.0, -3.0, -4.0, -6.0])


def pack_weight(w, fmt):
    k, n = w.shape
    w = f64(np.asarray(w, np.float32).astype(ml_dtypes.bfloat16)).reshape(k // 32, 32, n)
    amax = np.abs(w).max(1)
    if fmt == "e4m3":
        byte = np.frexp(amax)[1] - 1 + 127 - 7
    else:
        mant, ex = np.frexp(amax / 6.0)
        byte = np.where(mant > 0.5, ex, ex - 1) + 127
    byte = np.clip(np.where(amax > 0, byte, 1), 1, 254)
    scaled = (w * np.exp2(127.0 - byte)[:, None, :]).reshape(k, n).astype(np.float32)
    by_word = np.ascontiguousarray(scaled.reshape(k // 512, 128, 4, n).transpose(0, 1, 3, 2))
    if fmt == "e4m3":
        words = by_word.astype(ml_dtypes.float8_e4m3fn).view(np.uint8)
    else:
        c = by_word.astype(ml_dtypes.float4_e2m1fn).view(np.uint8) & 0xF
        words = (c[..., 0::2] | (c[..., 1::2] << 4)).reshape(k // 512, 128, 2 * n)
    return np.ascontiguousarray(words), np.ascontiguousarray(byte.astype(np.uint8).reshape(k // 512, 16, n))


def unpack_weight(words, scales, fmt):
    g, _, n = scales.shape
    words = np.ascontiguousarray(words).reshape(g, 128, n, -1)
    if fmt == "e4m3":
        vals = words.view(ml_dtypes.float8_e4m3fn).astype(np.float64)
    else:
        nib = np.empty((g, 128, n, 4), np.uint8)
        nib[..., 0::2] = words & 0xF
        nib[..., 1::2] = words >> 4
        vals = E2M1[nib]
    vals = vals * np.repeat(np.exp2(scales.astype(np.float64) - 127.0), 8, axis=1)[..., None]
    return vals.transpose(0, 1, 3, 2).reshape(g * 512, n)


def sigmoid(v):
    return 1.0 / (1.0 + np.exp(-v))


D, E, T, I, Q, G = 512, 512, 2048, 512, 128, 32


def setup_inputs():
    n = np.random.standard_normal
    idx = np.random.permutation(T)[:I]
    fd = mx_kscale(D)
    fe = mx_kscale(E)
    keysp = pack_weight(n((D, T)) / fd[:, None], "e4m3")
    valsp = pack_weight(n((E, T)) / fe[:, None], "e4m3")
    return {
        "query": (n((D, Q)) * 0.8 / np.sqrt(D) * fd[:, None]).astype(np.float32),
        "keys_words": keysp[0],
        "keys_scales": keysp[1],
        "th": (np.random.uniform(-0.5, 0.5, (Q, 1))).astype(np.float32),
        "sharp": (np.random.uniform(1.0, 3.0, (Q, 1))).astype(np.float32),
        "gout": (n((E, Q)) * 1 / np.sqrt(E) * fe[:, None]).astype(np.float32),
        "vals_words": valsp[0],
        "vals_scales": valsp[1],
        "old": (0.5 * n((Q, T))).astype(np.float32),
        "offs": striped(idx),
    }


def reference(query, keys_words, keys_scales, th, sharp, gout, vals_words, vals_scales, old, offs):
    idx = unstriped(offs)
    keysu = unpack_weight(keys_words, keys_scales, "e4m3")
    valsu = unpack_weight(vals_words, vals_scales, "e4m3")
    queryq = mxq(f64(query), 0, "e4m3")
    keysidxg = keysu[:, idx]
    a = queryq.T @ keysidxg
    s = a.reshape(Q, G, I // G).mean(axis=2) * f64(sharp)
    p = np.exp(s - np.max(s, axis=1, keepdims=True))
    z = np.sum(p, axis=1, keepdims=True)
    r = p / z
    rr = np.repeat(r, I // G, axis=1)
    goutq = mxq(f64(gout), 0, "e4m3")
    valsidxg = valsu[:, idx]
    c0 = goutq.T @ valsidxg
    drr = c0 * sigmoid(a - f64(th))
    dr = drr.reshape(Q, G, I // G).sum(axis=2)
    dz = np.sum(dr * p / np.square(z) * (-1.0), axis=1, keepdims=True)
    dp = dr / z + dz
    ds = dp * p
    e1 = ds * f64(sharp) / 16.0
    r1 = np.repeat(e1, I // G, axis=1)
    da = c0 * rr * sigmoid(a - f64(th)) * (1.0 - sigmoid(a - f64(th))) + r1
    gs = da * 32.0
    gf = np.zeros((Q, T))
    gf[:, idx] = gs
    y = f64(old) + gf
    return y

@@ -1,0 +1,161 @@
+import math
+from contextlib import ExitStack
+
+import concourse.mybir as mybir
+
+F32 = mybir.dt.float32
+BF16 = mybir.dt.bfloat16
+I32 = mybir.dt.int32
+U32 = mybir.dt.uint32
+U16 = mybir.dt.uint16
+U8 = mybir.dt.uint8
+FP8X4 = mybir.dt.float8_e4m3fn_x4
+ALU = mybir.AluOpType
+ACT = mybir.ActivationFunctionType
+AXIS_X = mybir.AxisListType.X
+
+P = 128
+PACK = 4
+POOL = 2048
+SLOTS = 512
+ROWS = 128
+PAGE = 16
+PAGES = SLOTS // PAGE
+HALF = SLOTS // 2
+VALS_SCALE_ROW = 4
+STORE_WIDTHS = (256, 512, 512, 512, 256)
+
+FLOPS = 2 * 2 * 512 * ROWS * SLOTS
+
+
+def tile_attend_bpagetimessigmoid_s_kernel(tc, query, keys_words, keys_scales, th, sharp, gout, vals_words, vals_scales, old, offs, out):
+    nc = tc.nc
+
+    def by_page(ap):
+        return ap.rearrange("p (g i) -> p g i", i=PAGE)
+
+    def spread(per_page):
+        return per_page.unsqueeze(2).to_broadcast([P, PAGES, PAGE])
+
+    def interleave_views(grouped, raw):
+        return (grouped[:].rearrange("p (c i) t -> p c t i", i=PACK), raw[:].rearrange("p t (c i) -> p c t i", i=PACK))
+
+    def load_scale_rows(engine, plane, scales, j, first_row):
+        engine.dma_start(out=plane[first_row + j : P : 32, :].bitcast(I32), in_=scales[0].bitcast(I32)[j:16:PACK, :])
+
+    with ExitStack() as ctx:
+        keep = ctx.enter_context(tc.tile_pool(name="keep", bufs=1))
+        psum = ctx.enter_context(tc.psum_pool(name="psum", bufs=1))
+
+        offsets = keep.tile([P, SLOTS // 16], U16, name="offsets")
+        nc.sync.dma_start(offsets[:], offs)
+
+        key_plane = keep.tile([P, POOL], U8, name="key_plane", tag="slot_d", align_bytes=64)
+        val_plane = keep.tile([P, POOL], U8, name="val_plane", tag="slot_e", align_bytes=64)
+        nc.vector.memset(key_plane[:].bitcast(I32), 0)
+        nc.vector.memset(val_plane[:].bitcast(I32), 0)
+
+        q_raw = keep.tile([P, PACK, ROWS], F32, name="q_raw", tag="slot_c", align_bytes=64)
+        g_raw = keep.tile([P, PACK, ROWS], F32, name="g_raw")
+        key_pool = keep.tile([P, POOL], U32, name="key_pool", tag="slot_b", align_bytes=64)
+        nc.sync.dma_start(out=q_raw[:], in_=query.rearrange("(p j) w -> p j w", j=PACK))
+        nc.sync.dma_start(out=g_raw[:], in_=gout.rearrange("(p j) w -> p j w", j=PACK))
+        nc.sync.dma_start(out=key_pool[:].bitcast(I32), in_=keys_words[0].rearrange("p n t -> p (n t)").bitcast(I32))
+        for j in range(PACK):
+            load_scale_rows(nc.scalar, key_plane, keys_scales, j, 0)
+        for j in range(PACK):
+            load_scale_rows(nc.scalar if j < 2 else nc.gpsimd, val_plane, vals_scales, j, VALS_SCALE_ROW)
+        th_col = keep.tile([P, 1], F32, name="th_col")
+        sharp_col = keep.tile([P, 1], F32, name="sharp_col")
+        nc.gpsimd.dma_start(out=th_col[:], in_=th)
+        nc.gpsimd.dma_start(out=sharp_col[:], in_=sharp)
+
+        q_bf = keep.tile([P, ROWS, PACK], BF16, name="q_bf", tag="slot_a", align_bytes=64)
+        g_bf = keep.tile([P, ROWS, PACK], BF16, name="g_bf", align_bytes=64)
+        q_codes = keep.tile([P, ROWS], U32, name="q_codes", align_bytes=64)
+        q_scales = keep.tile([P, ROWS], U8, name="q_scales", align_bytes=64)
+        g_scales = keep.tile([P, ROWS], U8, name="g_scales", align_bytes=64)
+        dst, src = interleave_views(q_bf, q_raw)
+        nc.vector.tensor_copy(out=dst, in_=src)
+        dst, src = interleave_views(g_bf, g_raw)
+        nc.scalar.activation(out=dst, in_=src, func=ACT.Copy)
+
+        nc.vector.quantize_mx(out=q_codes[:].bitcast(FP8X4), scales=q_scales[:], in_=q_bf[:].rearrange("p w j -> p (w j)"))
+        val_pool = keep.tile([P, POOL], U32, name="val_pool", tag="slot_a", align_bytes=64)
+        nc.sync.dma_start(out=val_pool[:].bitcast(I32), in_=vals_words[0].rearrange("p n t -> p (n t)").bitcast(I32))
+
+        key_scale = keep.tile([P, SLOTS], U8, name="key_scale", tag="slot_c", align_bytes=64)
+        nc.vector.tensor_copy(key_scale[:], key_plane[:].indirect(offsets[:]))
+        val_scale = keep.tile([P, SLOTS], U8, name="val_scale", tag="slot_d", align_bytes=64)
+        nc.vector.tensor_copy(val_scale[:], val_plane[:].indirect(offsets[:]))
+
+        half_th = keep.tile([P, 1], F32, name="half_th")
+        logit_scale = keep.tile([P, 1], F32, name="logit_scale")
+        nc.gpsimd.tensor_scalar(out=half_th[:], in0=th_col[:], scalar1=-0.5, scalar2=0.0, op0=ALU.mult, op1=ALU.add)
+        nc.gpsimd.tensor_scalar(out=logit_scale[:], in0=sharp_col[:], scalar1=-1.0 / PAGE, scalar2=0.0, op0=ALU.mult, op1=ALU.add)
+
+        halves = [slice(h * HALF, (h + 1) * HALF) for h in range(2)]
+        lists = [offsets[:, h * (HALF // 16) : (h + 1) * (HALF // 16)] for h in range(2)]
+
+        key_words = keep.tile([P, SLOTS], U32, name="key_words", tag="slot_e", align_bytes=64)
+        score = [psum.tile([ROWS, HALF], F32, name="score%d" % h) for h in range(2)]
+        for h in range(2):
+            nc.vector.tensor_copy(key_words[:, halves[h]], key_pool[:].indirect(lists[h]))
+            nc.tensor.matmul_mx(out=score[h][:], lhsT=q_codes[:].bitcast(FP8X4), lhsT_scale=q_scales[:],
+                                rhs=key_words[:, halves[h]].bitcast(FP8X4), rhs_scale=key_scale[:, halves[h]], start=True, stop=True)
+
+        g_codes = keep.tile([P, ROWS], U32, name="g_codes", tag="slot_b", align_bytes=64)
+        nc.vector.quantize_mx(out=g_codes[:].bitcast(FP8X4), scales=g_scales[:], in_=g_bf[:].rearrange("p w j -> p (w j)"))
+        placed = keep.tile([P, POOL], F32, name="placed", tag="slot_e", align_bytes=64)
+        nc.gpsimd.memset(placed[:], 0.0)
+
+        page_sum = keep.tile([P, PAGES], F32, name="page_sum")
+        tanh = keep.tile([P, SLOTS], F32, name="tanh")
+        for h in range(2):
+            nc.vector.tensor_reduce(out=page_sum[:, h * (PAGES // 2) : (h + 1) * (PAGES // 2)], in_=by_page(score[h][:]), axis=AXIS_X, op=ALU.add)
+            nc.scalar.activation(out=tanh[:, halves[h]], in_=score[h][:], func=ACT.Tanh, scale=0.5, bias=half_th[:])
+        neg_logit = keep.tile([P, PAGES], F32, name="neg_logit")
+        neg_max = keep.tile([P, 1], F32, name="neg_max")
+        nc.vector.tensor_scalar(out=neg_logit[:], in0=page_sum[:], scalar1=logit_scale[:], scalar2=None, op0=ALU.mult, op1=ALU.min, accum_out=neg_max[:])
+        p_exp = keep.tile([P, PAGES], F32, name="p_exp")
+        z = keep.tile([P, 1], F32, name="z")
+        nc.scalar.activation(out=p_exp[:], in_=neg_logit[:], func=ACT.Exp, scale=-1.0, bias=neg_max[:], accum_out=z[:])
+        gate = keep.tile([P, SLOTS], F32, name="gate")
+        tanh_sq = keep.tile([P, SLOTS], F32, name="tanh_sq")
+        share = keep.tile([P, SLOTS], F32, name="share")
+        nc.scalar.activation(out=gate[:], in_=tanh[:], func=ACT.Identity, scale=sharp_col[:], bias=sharp_col[:])
+        nc.scalar.activation(out=tanh_sq[:], in_=tanh[:], func=ACT.Square, scale=math.sqrt(8.0))
+
+        val_words = keep.tile([P, SLOTS], U32, name="val_words", tag="slot_f", align_bytes=64)
+        c0 = [psum.tile([ROWS, HALF], F32, name="c0_%d" % h) for h in range(2)]
+        for h in range(2):
+            nc.vector.tensor_copy(val_words[:, halves[h]], val_pool[:].indirect(lists[h]))
+            nc.tensor.matmul_mx(out=c0[h][:], lhsT=g_codes[:].bitcast(FP8X4), lhsT_scale=g_scales[:],
+                                rhs=val_words[:, halves[h]].bitcast(FP8X4), rhs_scale=val_scale[VALS_SCALE_ROW:P, halves[h]], start=True, stop=True)
+
+        inv_z = keep.tile([P, 1], F32, name="inv_z", tag="slot_a", align_bytes=64)
+        nc.vector.reciprocal(out=inv_z[:], in_=z[:])
+        nc.scalar.activation(out=by_page(share[:]), in_=spread(p_exp[:]), func=ACT.Copy, scale=inv_z[:])
+        total = keep.tile([P, POOL], F32, name="total", tag="slot_f", align_bytes=64)
+        nc.sync.dma_start(out=total[:], in_=old)
+
+        gated = keep.tile([P, SLOTS], F32, name="gated")
+        neg_slope = keep.tile([P, SLOTS], F32, name="neg_slope")
+        for h in range(2):
+            nc.vector.tensor_tensor(out=gated[:, halves[h]], in0=gate[:, halves[h]], in1=c0[h][:], op=ALU.mult)
+            nc.vector.scalar_tensor_tensor(out=neg_slope[:, halves[h]], in0=tanh_sq[:, halves[h]], scalar=8.0, in1=c0[h][:], op0=ALU.subtract, op1=ALU.mult)
+        page_grad = keep.tile([P, PAGES], F32, name="page_grad")
+        nc.vector.tensor_reduce(out=page_grad[:], in_=by_page(gated[:]), axis=AXIS_X, op=ALU.add)
+        weighted = keep.tile([P, PAGES], F32, name="weighted")
+        mean_grad = keep.tile([P, 1], F32, name="mean_grad")
+        nc.vector.scalar_tensor_tensor(out=weighted[:], in0=page_grad[:], scalar=inv_z[:], in1=p_exp[:], op0=ALU.mult, op1=ALU.mult, accum_out=mean_grad[:])
+        inner = keep.tile([P, SLOTS], F32, name="inner")
+        nc.vector.scalar_tensor_tensor(out=by_page(inner[:]), in0=spread(page_grad[:]), scalar=mean_grad[:], in1=by_page(neg_slope[:]), op0=ALU.subtract, op1=ALU.subtract)
+        nc.vector.tensor_tensor(placed[:].indirect(offsets[:]), inner[:], share[:], ALU.mult)
+
+        start = 0
+        for n, width in enumerate(STORE_WIDTHS):
+            cols = slice(start, start + width)
+            nc.vector.tensor_tensor(out=total[:, cols], in0=total[:, cols], in1=placed[:, cols], op=ALU.add)
+            (nc.sync if n % 2 == 0 else nc.scalar).dma_start(out=out[:, cols], in_=total[:, cols])
+            start = start + width

@@ -60,15 +60,15 @@ def tile_attend_bpagetimessigmoid_s_kernel(tc, query, keys_words, keys_scales, t
         key_pool = keep.tile([P, POOL], U32, name="key_pool", tag="slot_b", align_bytes=64)
         nc.sync.dma_start(out=q_raw[:], in_=query.rearrange("(p j) w -> p j w", j=PACK))
         nc.sync.dma_start(out=g_raw[:], in_=gout.rearrange("(p j) w -> p j w", j=PACK))
+        for j in range(PACK):
+            load_scale_rows(nc.sync, key_plane, keys_scales, j, 0)
         nc.sync.dma_start(out=key_pool[:].bitcast(I32), in_=keys_words[0].rearrange("p n t -> p (n t)").bitcast(I32))
-        for j in range(PACK):
-            load_scale_rows(nc.scalar, key_plane, keys_scales, j, 0)
-        for j in range(PACK):
-            load_scale_rows(nc.scalar if j < 2 else nc.gpsimd, val_plane, vals_scales, j, VALS_SCALE_ROW)
         th_col = keep.tile([P, 1], F32, name="th_col")
         sharp_col = keep.tile([P, 1], F32, name="sharp_col")
-        nc.gpsimd.dma_start(out=th_col[:], in_=th)
-        nc.gpsimd.dma_start(out=sharp_col[:], in_=sharp)
+        nc.sync.dma_start(out=th_col[:], in_=th)
+        nc.sync.dma_start(out=sharp_col[:], in_=sharp)
+        for j in range(PACK):
+            load_scale_rows(nc.sync, val_plane, vals_scales, j, VALS_SCALE_ROW)
 
         q_bf = keep.tile([P, ROWS, PACK], BF16, name="q_bf", tag="slot_a", align_bytes=64)
         g_bf = keep.tile([P, ROWS, PACK], BF16, name="g_bf", align_bytes=64)
@@ -86,40 +86,35 @@ def tile_attend_bpagetimessigmoid_s_kernel(tc, query, keys_words, keys_scales, t
 
         key_scale = keep.tile([P, SLOTS], U8, name="key_scale", tag="slot_c", align_bytes=64)
         nc.vector.tensor_copy(key_scale[:], key_plane[:].indirect(offsets[:]))
-        val_scale = keep.tile([P, SLOTS], U8, name="val_scale", tag="slot_d", align_bytes=64)
-        nc.vector.tensor_copy(val_scale[:], val_plane[:].indirect(offsets[:]))
+
+        g_codes = keep.tile([P, ROWS], U32, name="g_codes", align_bytes=64)
+        nc.vector.quantize_mx(out=g_codes[:].bitcast(FP8X4), scales=g_scales[:], in_=g_bf[:].rearrange("p w j -> p (w j)"))
 
         half_th = keep.tile([P, 1], F32, name="half_th")
         logit_scale = keep.tile([P, 1], F32, name="logit_scale")
-        nc.gpsimd.tensor_scalar(out=half_th[:], in0=th_col[:], scalar1=-0.5, scalar2=0.0, op0=ALU.mult, op1=ALU.add)
-        nc.gpsimd.tensor_scalar(out=logit_scale[:], in0=sharp_col[:], scalar1=-1.0 / PAGE, scalar2=0.0, op0=ALU.mult, op1=ALU.add)
+        nc.scalar.activation(out=half_th[:], in_=th_col[:], func=ACT.Copy, scale=-0.5)
+        nc.scalar.activation(out=logit_scale[:], in_=sharp_col[:], func=ACT.Copy, scale=-1.0 / PAGE)
 
         halves = [slice(h * HALF, (h + 1) * HALF) for h in range(2)]
         lists = [offsets[:, h * (HALF // 16) : (h + 1) * (HALF // 16)] for h in range(2)]
 
-        key_words = keep.tile([P, SLOTS], U32, name="key_words", tag="slot_e", align_bytes=64)
+        key_words = keep.tile([P, SLOTS], U32, name="key_words", tag="slot_d", align_bytes=64)
         score = [psum.tile([ROWS, HALF], F32, name="score%d" % h) for h in range(2)]
         for h in range(2):
             nc.vector.tensor_copy(key_words[:, halves[h]], key_pool[:].indirect(lists[h]))
             nc.tensor.matmul_mx(out=score[h][:], lhsT=q_codes[:].bitcast(FP8X4), lhsT_scale=q_scales[:],
                                 rhs=key_words[:, halves[h]].bitcast(FP8X4), rhs_scale=key_scale[:, halves[h]], start=True, stop=True)
 
-        g_codes = keep.tile([P, ROWS], U32, name="g_codes", tag="slot_b", align_bytes=64)
-        nc.vector.quantize_mx(out=g_codes[:].bitcast(FP8X4), scales=g_scales[:], in_=g_bf[:].rearrange("p w j -> p (w j)"))
-        placed = keep.tile([P, POOL], F32, name="placed", tag="slot_e", align_bytes=64)
+        val_scale = keep.tile([P, SLOTS], U8, name="val_scale", tag="slot_b", align_bytes=64)
+        nc.vector.tensor_copy(val_scale[:], val_plane[:].indirect(offsets[:]))
+        placed = keep.tile([P, POOL], F32, name="placed", tag="slot_d", align_bytes=64)
         nc.gpsimd.memset(placed[:], 0.0)
 
-        page_sum = keep.tile([P, PAGES], F32, name="page_sum")
+        page_sum = keep.tile([P, PAGES], F32, name="page_sum", tag="slot_e", align_bytes=64)
         tanh = keep.tile([P, SLOTS], F32, name="tanh")
         for h in range(2):
-            nc.vector.tensor_reduce(out=page_sum[:, h * (PAGES // 2) : (h + 1) * (PAGES // 2)], in_=by_page(score[h][:]), axis=AXIS_X, op=ALU.add)
             nc.scalar.activation(out=tanh[:, halves[h]], in_=score[h][:], func=ACT.Tanh, scale=0.5, bias=half_th[:])
-        neg_logit = keep.tile([P, PAGES], F32, name="neg_logit")
-        neg_max = keep.tile([P, 1], F32, name="neg_max")
-        nc.vector.tensor_scalar(out=neg_logit[:], in0=page_sum[:], scalar1=logit_scale[:], scalar2=None, op0=ALU.mult, op1=ALU.min, accum_out=neg_max[:])
-        p_exp = keep.tile([P, PAGES], F32, name="p_exp")
-        z = keep.tile([P, 1], F32, name="z")
-        nc.scalar.activation(out=p_exp[:], in_=neg_logit[:], func=ACT.Exp, scale=-1.0, bias=neg_max[:], accum_out=z[:])
+            nc.vector.tensor_reduce(out=page_sum[:, h * (PAGES // 2) : (h + 1) * (PAGES // 2)], in_=by_page(score[h][:]), axis=AXIS_X, op=ALU.add)
         gate = keep.tile([P, SLOTS], F32, name="gate")
         tanh_sq = keep.tile([P, SLOTS], F32, name="tanh_sq")
         share = keep.tile([P, SLOTS], F32, name="share")
@@ -133,7 +128,13 @@ def tile_attend_bpagetimessigmoid_s_kernel(tc, query, keys_words, keys_scales, t
             nc.tensor.matmul_mx(out=c0[h][:], lhsT=g_codes[:].bitcast(FP8X4), lhsT_scale=g_scales[:],
                                 rhs=val_words[:, halves[h]].bitcast(FP8X4), rhs_scale=val_scale[VALS_SCALE_ROW:P, halves[h]], start=True, stop=True)
 
-        inv_z = keep.tile([P, 1], F32, name="inv_z", tag="slot_a", align_bytes=64)
+        neg_logit = keep.tile([P, PAGES], F32, name="neg_logit", tag="slot_a", align_bytes=64)
+        neg_max = keep.tile([P, 1], F32, name="neg_max")
+        nc.vector.tensor_scalar(out=neg_logit[:], in0=page_sum[:], scalar1=logit_scale[:], scalar2=None, op0=ALU.mult, op1=ALU.min, accum_out=neg_max[:])
+        p_exp = keep.tile([P, PAGES], F32, name="p_exp")
+        z = keep.tile([P, 1], F32, name="z")
+        nc.scalar.activation(out=p_exp[:], in_=neg_logit[:], func=ACT.Exp, scale=-1.0, bias=neg_max[:], accum_out=z[:])
+        inv_z = keep.tile([P, 1], F32, name="inv_z")
         nc.vector.reciprocal(out=inv_z[:], in_=z[:])
         nc.scalar.activation(out=by_page(share[:]), in_=spread(p_exp[:]), func=ACT.Copy, scale=inv_z[:])
         total = keep.tile([P, POOL], F32, name="total", tag="slot_f", align_bytes=64)

@@ -54,18 +54,20 @@ def tile_attend_bpagetimessigmoid_s_kernel(tc, query, keys_words, keys_scales, t
         val_plane = keep.tile([P, POOL], U8, name="val_plane", tag="slot_e", align_bytes=64)
         nc.vector.memset(key_plane[:].bitcast(I32), 0)
         nc.vector.memset(val_plane[:].bitcast(I32), 0)
+        placed = keep.tile([P, POOL], F32, name="placed")
+        nc.vector.memset(placed[:], 0.0)
 
         q_raw = keep.tile([P, PACK, ROWS], F32, name="q_raw", tag="slot_c", align_bytes=64)
         g_raw = keep.tile([P, PACK, ROWS], F32, name="g_raw")
         key_pool = keep.tile([P, POOL], U32, name="key_pool", tag="slot_b", align_bytes=64)
         nc.sync.dma_start(out=q_raw[:], in_=query.rearrange("(p j) w -> p j w", j=PACK))
-        nc.sync.dma_start(out=g_raw[:], in_=gout.rearrange("(p j) w -> p j w", j=PACK))
+        th_col = keep.tile([P, 1], F32, name="th_col")
+        nc.sync.dma_start(out=th_col[:], in_=th)
         for j in range(PACK):
             load_scale_rows(nc.sync, key_plane, keys_scales, j, 0)
         nc.sync.dma_start(out=key_pool[:].bitcast(I32), in_=keys_words[0].rearrange("p n t -> p (n t)").bitcast(I32))
-        th_col = keep.tile([P, 1], F32, name="th_col")
+        nc.sync.dma_start(out=g_raw[:], in_=gout.rearrange("(p j) w -> p j w", j=PACK))
         sharp_col = keep.tile([P, 1], F32, name="sharp_col")
-        nc.sync.dma_start(out=th_col[:], in_=th)
         nc.sync.dma_start(out=sharp_col[:], in_=sharp)
         for j in range(PACK):
             load_scale_rows(nc.sync, val_plane, vals_scales, j, VALS_SCALE_ROW)
@@ -77,8 +79,6 @@ def tile_attend_bpagetimessigmoid_s_kernel(tc, query, keys_words, keys_scales, t
         g_scales = keep.tile([P, ROWS], U8, name="g_scales", align_bytes=64)
         dst, src = interleave_views(q_bf, q_raw)
         nc.vector.tensor_copy(out=dst, in_=src)
-        dst, src = interleave_views(g_bf, g_raw)
-        nc.scalar.activation(out=dst, in_=src, func=ACT.Copy)
 
         nc.vector.quantize_mx(out=q_codes[:].bitcast(FP8X4), scales=q_scales[:], in_=q_bf[:].rearrange("p w j -> p (w j)"))
         val_pool = keep.tile([P, POOL], U32, name="val_pool", tag="slot_a", align_bytes=64)
@@ -87,9 +87,9 @@ def tile_attend_bpagetimessigmoid_s_kernel(tc, query, keys_words, keys_scales, t
         key_scale = keep.tile([P, SLOTS], U8, name="key_scale", tag="slot_c", align_bytes=64)
         nc.vector.tensor_copy(key_scale[:], key_plane[:].indirect(offsets[:]))
 
-        g_codes = keep.tile([P, ROWS], U32, name="g_codes", align_bytes=64)
-        nc.vector.quantize_mx(out=g_codes[:].bitcast(FP8X4), scales=g_scales[:], in_=g_bf[:].rearrange("p w j -> p (w j)"))
 
+        dst, src = interleave_views(g_bf, g_raw)
+        nc.scalar.activation(out=dst, in_=src, func=ACT.Copy)
         half_th = keep.tile([P, 1], F32, name="half_th")
         logit_scale = keep.tile([P, 1], F32, name="logit_scale")
         nc.scalar.activation(out=half_th[:], in_=th_col[:], func=ACT.Copy, scale=-0.5)
@@ -107,9 +107,9 @@ def tile_attend_bpagetimessigmoid_s_kernel(tc, query, keys_words, keys_scales, t
 
         val_scale = keep.tile([P, SLOTS], U8, name="val_scale", tag="slot_b", align_bytes=64)
         nc.vector.tensor_copy(val_scale[:], val_plane[:].indirect(offsets[:]))
-        placed = keep.tile([P, POOL], F32, name="placed", tag="slot_d", align_bytes=64)
-        nc.gpsimd.memset(placed[:], 0.0)
 
+        g_codes = keep.tile([P, ROWS], U32, name="g_codes", align_bytes=64)
+        nc.vector.quantize_mx(out=g_codes[:].bitcast(FP8X4), scales=g_scales[:], in_=g_bf[:].rearrange("p w j -> p (w j)"))
         page_sum = keep.tile([P, PAGES], F32, name="page_sum", tag="slot_e", align_bytes=64)
         tanh = keep.tile([P, SLOTS], F32, name="tanh")
         for h in range(2):

import math
from contextlib import ExitStack

import concourse.mybir as mybir

F32 = mybir.dt.float32
BF16 = mybir.dt.bfloat16
I32 = mybir.dt.int32
U32 = mybir.dt.uint32
U16 = mybir.dt.uint16
U8 = mybir.dt.uint8
FP8X4 = mybir.dt.float8_e4m3fn_x4
ALU = mybir.AluOpType
ACT = mybir.ActivationFunctionType
AXIS_X = mybir.AxisListType.X

P = 128
PACK = 4
POOL = 2048
SLOTS = 512
ROWS = 128
PAGE = 16
PAGES = SLOTS // PAGE
HALF = SLOTS // 2
VALS_SCALE_ROW = 4
STORE_WIDTHS = (256, 512, 512, 512, 256)

FLOPS = 2 * 2 * 512 * ROWS * SLOTS


def tile_attend_bpagetimessigmoid_s_kernel(tc, query, keys_words, keys_scales, th, sharp, gout, vals_words, vals_scales, old, offs, out):
    nc = tc.nc

    def by_page(ap):
        return ap.rearrange("p (g i) -> p g i", i=PAGE)

    def spread(per_page):
        return per_page.unsqueeze(2).to_broadcast([P, PAGES, PAGE])

    def interleave_views(grouped, raw):
        return (grouped[:].rearrange("p (c i) t -> p c t i", i=PACK), raw[:].rearrange("p t (c i) -> p c t i", i=PACK))

    def load_scale_rows(engine, plane, scales, j, first_row):
        engine.dma_start(out=plane[first_row + j : P : 32, :].bitcast(I32), in_=scales[0].bitcast(I32)[j:16:PACK, :])

    with ExitStack() as ctx:
        keep = ctx.enter_context(tc.tile_pool(name="keep", bufs=1))
        psum = ctx.enter_context(tc.psum_pool(name="psum", bufs=1))

        offsets = keep.tile([P, SLOTS // 16], U16, name="offsets")
        nc.sync.dma_start(offsets[:], offs)

        key_plane = keep.tile([P, POOL], U8, name="key_plane", tag="slot_d", align_bytes=64)
        val_plane = keep.tile([P, POOL], U8, name="val_plane", tag="slot_e", align_bytes=64)
        nc.vector.memset(key_plane[:].bitcast(I32), 0)
        nc.vector.memset(val_plane[:].bitcast(I32), 0)
        placed = keep.tile([P, POOL], F32, name="placed")
        nc.vector.memset(placed[:], 0.0)

        q_raw = keep.tile([P, PACK, ROWS], F32, name="q_raw", tag="slot_c", align_bytes=64)
        g_raw = keep.tile([P, PACK, ROWS], F32, name="g_raw")
        key_pool = keep.tile([P, POOL], U32, name="key_pool", tag="slot_b", align_bytes=64)
        nc.sync.dma_start(out=q_raw[:], in_=query.rearrange("(p j) w -> p j w", j=PACK))
        th_col = keep.tile([P, 1], F32, name="th_col")
        nc.sync.dma_start(out=th_col[:], in_=th)
        for j in range(PACK):
            load_scale_rows(nc.sync, key_plane, keys_scales, j, 0)
        nc.sync.dma_start(out=key_pool[:].bitcast(I32), in_=keys_words[0].rearrange("p n t -> p (n t)").bitcast(I32))
        nc.sync.dma_start(out=g_raw[:], in_=gout.rearrange("(p j) w -> p j w", j=PACK))
        sharp_col = keep.tile([P, 1], F32, name="sharp_col")
        nc.sync.dma_start(out=sharp_col[:], in_=sharp)
        for j in range(PACK):
            load_scale_rows(nc.sync, val_plane, vals_scales, j, VALS_SCALE_ROW)

        q_bf = keep.tile([P, ROWS, PACK], BF16, name="q_bf", tag="slot_a", align_bytes=64)
        g_bf = keep.tile([P, ROWS, PACK], BF16, name="g_bf", align_bytes=64)
        q_codes = keep.tile([P, ROWS], U32, name="q_codes", align_bytes=64)
        q_scales = keep.tile([P, ROWS], U8, name="q_scales", align_bytes=64)
        g_scales = keep.tile([P, ROWS], U8, name="g_scales", align_bytes=64)
        dst, src = interleave_views(q_bf, q_raw)
        nc.vector.tensor_copy(out=dst, in_=src)

        nc.vector.quantize_mx(out=q_codes[:].bitcast(FP8X4), scales=q_scales[:], in_=q_bf[:].rearrange("p w j -> p (w j)"))
        val_pool = keep.tile([P, POOL], U32, name="val_pool", tag="slot_a", align_bytes=64)
        nc.sync.dma_start(out=val_pool[:].bitcast(I32), in_=vals_words[0].rearrange("p n t -> p (n t)").bitcast(I32))

        key_scale = keep.tile([P, SLOTS], U8, name="key_scale", tag="slot_c", align_bytes=64)
        nc.vector.tensor_copy(key_scale[:], key_plane[:].indirect(offsets[:]))


        dst, src = interleave_views(g_bf, g_raw)
        nc.scalar.activation(out=dst, in_=src, func=ACT.Copy)
        half_th = keep.tile([P, 1], F32, name="half_th")
        logit_scale = keep.tile([P, 1], F32, name="logit_scale")
        nc.scalar.activation(out=half_th[:], in_=th_col[:], func=ACT.Copy, scale=-0.5)
        nc.scalar.activation(out=logit_scale[:], in_=sharp_col[:], func=ACT.Copy, scale=-1.0 / PAGE)

        halves = [slice(h * HALF, (h + 1) * HALF) for h in range(2)]
        lists = [offsets[:, h * (HALF // 16) : (h + 1) * (HALF // 16)] for h in range(2)]

        key_words = keep.tile([P, SLOTS], U32, name="key_words", tag="slot_d", align_bytes=64)
        score = [psum.tile([ROWS, HALF], F32, name="score%d" % h) for h in range(2)]
        for h in range(2):
            nc.vector.tensor_copy(key_words[:, halves[h]], key_pool[:].indirect(lists[h]))
            nc.tensor.matmul_mx(out=score[h][:], lhsT=q_codes[:].bitcast(FP8X4), lhsT_scale=q_scales[:],
                                rhs=key_words[:, halves[h]].bitcast(FP8X4), rhs_scale=key_scale[:, halves[h]], start=True, stop=True)

        val_scale = keep.tile([P, SLOTS], U8, name="val_scale", tag="slot_b", align_bytes=64)
        nc.vector.tensor_copy(val_scale[:], val_plane[:].indirect(offsets[:]))

        g_codes = keep.tile([P, ROWS], U32, name="g_codes", align_bytes=64)
        nc.vector.quantize_mx(out=g_codes[:].bitcast(FP8X4), scales=g_scales[:], in_=g_bf[:].rearrange("p w j -> p (w j)"))
        page_sum = keep.tile([P, PAGES], F32, name="page_sum", tag="slot_e", align_bytes=64)
        tanh = keep.tile([P, SLOTS], F32, name="tanh")
        for h in range(2):
            nc.scalar.activation(out=tanh[:, halves[h]], in_=score[h][:], func=ACT.Tanh, scale=0.5, bias=half_th[:])
            nc.vector.tensor_reduce(out=page_sum[:, h * (PAGES // 2) : (h + 1) * (PAGES // 2)], in_=by_page(score[h][:]), axis=AXIS_X, op=ALU.add)
        gate = keep.tile([P, SLOTS], F32, name="gate")
        tanh_sq = keep.tile([P, SLOTS], F32, name="tanh_sq")
        share = keep.tile([P, SLOTS], F32, name="share")
        nc.scalar.activation(out=gate[:], in_=tanh[:], func=ACT.Identity, scale=sharp_col[:], bias=sharp_col[:])
        nc.scalar.activation(out=tanh_sq[:], in_=tanh[:], func=ACT.Square, scale=math.sqrt(8.0))

        val_words = keep.tile([P, SLOTS], U32, name="val_words", tag="slot_f", align_bytes=64)
        c0 = [psum.tile([ROWS, HALF], F32, name="c0_%d" % h) for h in range(2)]
        for h in range(2):
            nc.vector.tensor_copy(val_words[:, halves[h]], val_pool[:].indirect(lists[h]))
            nc.tensor.matmul_mx(out=c0[h][:], lhsT=g_codes[:].bitcast(FP8X4), lhsT_scale=g_scales[:],
                                rhs=val_words[:, halves[h]].bitcast(FP8X4), rhs_scale=val_scale[VALS_SCALE_ROW:P, halves[h]], start=True, stop=True)

        neg_logit = keep.tile([P, PAGES], F32, name="neg_logit", tag="slot_a", align_bytes=64)
        neg_max = keep.tile([P, 1], F32, name="neg_max")
        nc.vector.tensor_scalar(out=neg_logit[:], in0=page_sum[:], scalar1=logit_scale[:], scalar2=None, op0=ALU.mult, op1=ALU.min, accum_out=neg_max[:])
        p_exp = keep.tile([P, PAGES], F32, name="p_exp")
        z = keep.tile([P, 1], F32, name="z")
        nc.scalar.activation(out=p_exp[:], in_=neg_logit[:], func=ACT.Exp, scale=-1.0, bias=neg_max[:], accum_out=z[:])
        inv_z = keep.tile([P, 1], F32, name="inv_z")
        nc.vector.reciprocal(out=inv_z[:], in_=z[:])
        nc.scalar.activation(out=by_page(share[:]), in_=spread(p_exp[:]), func=ACT.Copy, scale=inv_z[:])
        total = keep.tile([P, POOL], F32, name="total", tag="slot_f", align_bytes=64)
        nc.sync.dma_start(out=total[:], in_=old)

        gated = keep.tile([P, SLOTS], F32, name="gated")
        neg_slope = keep.tile([P, SLOTS], F32, name="neg_slope")
        for h in range(2):
            nc.vector.tensor_tensor(out=gated[:, halves[h]], in0=gate[:, halves[h]], in1=c0[h][:], op=ALU.mult)
            nc.vector.scalar_tensor_tensor(out=neg_slope[:, halves[h]], in0=tanh_sq[:, halves[h]], scalar=8.0, in1=c0[h][:], op0=ALU.subtract, op1=ALU.mult)
        page_grad = keep.tile([P, PAGES], F32, name="page_grad")
        nc.vector.tensor_reduce(out=page_grad[:], in_=by_page(gated[:]), axis=AXIS_X, op=ALU.add)
        weighted = keep.tile([P, PAGES], F32, name="weighted")
        mean_grad = keep.tile([P, 1], F32, name="mean_grad")
        nc.vector.scalar_tensor_tensor(out=weighted[:], in0=page_grad[:], scalar=inv_z[:], in1=p_exp[:], op0=ALU.mult, op1=ALU.mult, accum_out=mean_grad[:])
        inner = keep.tile([P, SLOTS], F32, name="inner")
        nc.vector.scalar_tensor_tensor(out=by_page(inner[:]), in0=spread(page_grad[:]), scalar=mean_grad[:], in1=by_page(neg_slope[:]), op0=ALU.subtract, op1=ALU.subtract)
        nc.vector.tensor_tensor(placed[:].indirect(offsets[:]), inner[:], share[:], ALU.mult)

        start = 0
        for n, width in enumerate(STORE_WIDTHS):
            cols = slice(start, start + width)
            nc.vector.tensor_tensor(out=total[:, cols], in0=total[:, cols], in1=placed[:, cols], op=ALU.add)
            (nc.sync if n % 2 == 0 else nc.scalar).dma_start(out=out[:, cols], in_=total[:, cols])
            start = start + width
